import numpy as np
import ml_dtypes


def mxq(x, axis, fmt="e4m3"):
    dtype, down = {"e4m3": (ml_dtypes.float8_e4m3fn, 7), "e5m2": (ml_dtypes.float8_e5m2, 14)}[fmt]
    v = np.moveaxis(np.asarray(x, np.float32).astype(ml_dtypes.bfloat16).astype(np.float64), axis, -1)
    blocks = v.reshape(v.shape[:-1] + (-1, 32))
    amax = np.abs(blocks).max(-1, keepdims=True)
    byte = np.maximum(np.where(amax > 0, np.frexp(amax)[1] - 1 + 127, 0) - down, 1)
    scale = np.exp2(byte - 127.0)
    codes = (blocks / scale).astype(np.float32).astype(dtype).astype(np.float64)
    return np.moveaxis((codes * scale).reshape(v.shape), -1, axis)


WIDE = False


def mx_kscale(k):
    if not WIDE:
        return np.ones(k)
    levels = np.array([10, -10, 5, -5, 0])
    if k % 512:
        return np.exp2(np.random.permutation(np.resize(levels, k // 32))).repeat(32)
    a = np.empty((k // 512, 16))
    for p in range(k // 512):
        a[p, :8] = np.random.permutation(np.resize(levels, 8))
        for g in range(8):
            far = levels[np.abs(levels - a[p, g]) >= 10]
            a[p, g + 8] = far[np.random.randint(len(far))]
    return np.exp2(a.ravel()).repeat(32)


def f64(x):
    return np.asarray(x).astype(np.float64)


def striped(idx):
    return np.tile(np.asarray(idx).reshape(-1, 16).T, (8, 1)).astype(np.uint16)


def unstriped(offs):
    return offs[:16].T.reshape(-1).astype(np.int64)


E2M1 = np.array([0.0, 0.5, 1.0, 1.5, 2.0, 3.0, 4.0, 6.0, -0.0, -0.5, -1.0, -1.5, -2.0, -3.0, -4.0, -6.0])


def pack_weight(w, fmt):
    k, n = w.shape
    w = f64(np.asarray(w, np.float32).astype(ml_dtypes.bfloat16)).reshape(k // 32, 32, n)
    amax = np.abs(w).max(1)
    if fmt == "e4m3":
        byte = np.frexp(amax)[1] - 1 + 127 - 7
    else:
        mant, ex = np.frexp(amax / 6.0)
        byte = np.where(mant > 0.5, ex, ex - 1) + 127
    byte = np.clip(np.where(amax > 0, byte, 1), 1, 254)
    scaled = (w * np.exp2(127.0 - byte)[:, None, :]).reshape(k, n).astype(np.float32)
    by_word = np.ascontiguousarray(scaled.reshape(k // 512, 128, 4, n).transpose(0, 1, 3, 2))
    if fmt == "e4m3":
        words = by_word.astype(ml_dtypes.float8_e4m3fn).view(np.uint8)
    else:
        c = by_word.astype(ml_dtypes.float4_e2m1fn).view(np.uint8) & 0xF
        words = (c[..., 0::2] | (c[..., 1::2] << 4)).reshape(k // 512, 128, 2 * n)
    return np.ascontiguousarray(words), np.ascontiguousarray(byte.astype(np.uint8).reshape(k // 512, 16, n))


def unpack_weight(words, scales, fmt):
    g, _, n = scales.shape
    words = np.ascontiguousarray(words).reshape(g, 128, n, -1)
    if fmt == "e4m3":
        vals = words.view(ml_dtypes.float8_e4m3fn).astype(np.float64)
    else:
        nib = np.empty((g, 128, n, 4), np.uint8)
        nib[..., 0::2] = words & 0xF
        nib[..., 1::2] = words >> 4
        vals = E2M1[nib]
    vals = vals * np.repeat(np.exp2(scales.astype(np.float64) - 127.0), 8, axis=1)[..., None]
    return vals.transpose(0, 1, 3, 2).reshape(g * 512, n)


D, T, I, Q, U = 512, 1024, 256, 512, 1024


def setup_inputs():
    n = np.random.standard_normal
    idx = np.random.permutation(T)[:I]
    idx2 = np.random.permutation(T)[:I]
    idx4 = np.random.permutation(U)[:Q]
    fd = mx_kscale(D)
    fq = mx_kscale(Q)
    qpoolp = pack_weight(n((D, U)) * 0.03 * fd[:, None], "e4m3")
    return {
        "keys": (n((D, T))).astype(np.float32),
        "qpool_words": qpoolp[0],
        "qpool_scales": qpoolp[1],
        "ksc": (np.random.uniform(0.5, 2.0, (D, 1)) / fd[:, None]).astype(np.float32),
        "qs": (np.random.uniform(16.0, 64.0, (Q, 1)) * fq[:, None]).astype(np.float32),
        "target": (np.random.uniform(0.0, 0.008, (Q, I))).astype(np.float32),
        "qrows": (n((Q, D)) / fq[:, None]).astype(np.float32),
        "lift": (n((D, T)) * 0.4).astype(np.float32),
        "sg": (np.random.uniform(0.5, 2.0, (1, I))).astype(np.float32),
        "old": (n((D, T)) * 1.0).astype(np.float32),
        "fade": (np.random.uniform(0.5, 1.0, (1, T))).astype(np.float32),
        "offs": striped(idx),
        "offs2": striped(idx2),
        "offs4": striped(idx4),
    }


def reference(keys, qpool_words, qpool_scales, ksc, qs, target, qrows, lift, sg, old, fade, offs, offs2, offs4):
    idx = unstriped(offs)
    idx2 = unstriped(offs2)
    idx4 = unstriped(offs4)
    qpoolu = unpack_weight(qpool_words, qpool_scales, "e4m3")
    l1 = np.exp(f64(lift)[:, idx2])
    x1 = f64(keys)[:, idx] * l1
    vp = np.tanh(x1)
    kp = vp * f64(ksc)
    qpoolidx4g = qpoolu[:, idx4]
    kpq = mxq(kp, 0, "e4m3")
    a = qpoolidx4g.T @ kpq
    p = np.exp(a - np.max(a, axis=1, keepdims=True))
    ds = (p / np.sum(p, axis=1, keepdims=True) - f64(target)) * f64(qs)
    qrowsq = mxq(f64(qrows), 0, "e4m3")
    dsq = mxq(ds, 0, "e4m3")
    c0 = qrowsq.T @ dsq
    dx1 = c0 * (1.0 - np.square(vp))
    gs = dx1 * f64(sg)
    gf = np.zeros((D, T))
    gf[:, idx] = gs
    y = f64(old) * f64(fade) + gf
    return y

@@ -1,0 +1,194 @@
+from contextlib import ExitStack
+
+import concourse.mybir as mybir
+from concourse.masks import make_identity
+
+D, T, I, Q, U = 512, 1024, 256, 512, 1024
+FLOPS = 2 * 2 * D * Q * I
+
+F32 = mybir.dt.float32
+BF16 = mybir.dt.bfloat16
+I32 = mybir.dt.int32
+U32 = mybir.dt.uint32
+U16 = mybir.dt.uint16
+U8 = mybir.dt.uint8
+FP8X4 = mybir.dt.float8_e4m3fn_x4
+ACT = mybir.ActivationFunctionType
+ALU = mybir.AluOpType
+AXIS_X = mybir.AxisListType.X
+
+P = 128
+PACK = 4
+BANK = 512
+CHUNKS = T // P
+
+
+def tile_attend_bklifted_s_kernel(tc, keys, qpool_words, qpool_scales, ksc, qs, target, qrows, lift, sg, old, fade,
+                                   offs, offs2, offs4, out):
+    nc = tc.nc
+    with ExitStack() as ctx:
+        lists = ctx.enter_context(tc.tile_pool(name="lists", bufs=1))
+        sb = ctx.enter_context(tc.tile_pool(name="sb", bufs=1))
+        psum = ctx.enter_context(tc.psum_pool(name="psum", bufs=1))
+
+        offs_sb = lists.tile([P, I // 16], U16, name="offs_sb")
+        offs2_sb = lists.tile([P, I // 16], U16, name="offs2_sb")
+        offs4_sb = lists.tile([P, Q // 16], U16, name="offs4_sb")
+
+        scale_pool = sb.tile([P, U], U8, name="scale_pool", align_bytes=64)
+        nc.gpsimd.memset(scale_pool[:].bitcast(I32), 0)
+        rows = sb.tile([P, P], F32, name="rows")
+        nc.gpsimd.memset(rows[:], 0.0)
+        ident = sb.tile([P, P], F32, name="ident")
+        make_identity(nc, ident[:])
+        gf = [sb.tile([P, T], F32, name=f"gf{j}") for j in range(PACK)]
+        for j in range(PACK):
+            nc.vector.memset(gf[j][:], 0.0)
+
+        lift_planes = lift.rearrange("(p j) t -> j p t", j=PACK)
+        keys_planes = keys.rearrange("(p j) t -> j p t", j=PACK)
+        lift_sb = [sb.tile([P, T], F32, name=f"lift{j}") for j in range(PACK)]
+        keys_sb = [sb.tile([P, T], F32, name=f"keys{j}") for j in range(PACK)]
+        ksc_sb = sb.tile([P, PACK], F32, name="ksc_sb")
+        qs_sb = sb.tile([P, PACK], F32, name="qs_sb")
+        nc.sync.dma_start(out=lift_sb[0][:], in_=lift_planes[0])
+        nc.sync.dma_start(offs2_sb[:], offs2)
+        nc.sync.dma_start(offs4_sb[:], offs4)
+        for quad in range(4):
+            nc.sync.dma_start(out=scale_pool[32 * quad:32 * quad + 4, :].bitcast(I32),
+                              in_=qpool_scales[0][4 * quad:4 * quad + 4, :].bitcast(I32))
+        nc.sync.dma_start(out=keys_sb[0][:], in_=keys_planes[0])
+        nc.sync.dma_start(offs_sb[:], offs)
+        nc.sync.dma_start(out=ksc_sb[:], in_=ksc.rearrange("(p j) o -> p (j o)", j=PACK))
+        for j in range(1, PACK):
+            nc.sync.dma_start(out=lift_sb[j][:], in_=lift_planes[j])
+            nc.sync.dma_start(out=keys_sb[j][:], in_=keys_planes[j])
+            if j == 1:
+                nc.sync.dma_start(out=rows[0:CHUNKS, :], in_=fade.rearrange("o (c p) -> (o c) p", p=P))
+                nc.sync.dma_start(out=rows[CHUNKS:CHUNKS + I // P, :], in_=sg.rearrange("o (c p) -> (o c) p", p=P))
+        word_pool = sb.tile([P, U], U32, name="word_pool", align_bytes=64)
+        nc.sync.dma_start(out=word_pool[:].bitcast(I32),
+                          in_=qpool_words[0].rearrange("p u r -> p (u r)").bitcast(I32))
+        nc.sync.dma_start(out=qs_sb[:], in_=qs.rearrange("(p r) o -> p (r o)", r=PACK))
+        target_sb = sb.tile([P, PACK, I], F32, name="target_sb")
+        nc.sync.dma_start(out=target_sb[:], in_=target.rearrange("(p r) i -> p r i", r=PACK))
+        qrows_sb = sb.tile([P, PACK, D], F32, name="qrows_sb")
+        nc.sync.dma_start(out=qrows_sb[:], in_=qrows.rearrange("(p r) d -> p r d", r=PACK))
+        old_rows = old.rearrange("(p j) t -> p j t", j=PACK)
+        old_sb = [sb.tile([P, PACK, BANK], F32, name=f"old{h}") for h in range(T // BANK)]
+        for h in range(T // BANK):
+            nc.sync.dma_start(out=old_sb[h][:], in_=old_rows[:, :, h * BANK:(h + 1) * BANK])
+
+        cols_ps = psum.tile([P, BANK], F32, name="cols_ps", tag="score", bufs=4)
+        nc.tensor.transpose(cols_ps[:, 0:P], rows[:], ident[:])
+        cols = sb.tile([P, 16], F32, name="cols")
+        nc.scalar.copy(out=cols[:], in_=cols_ps[:, 0:16])
+        sg_ps = psum.tile([P, BANK], F32, name="sg_ps", tag="score", bufs=4)
+        for c in range(I // P):
+            nc.tensor.transpose(sg_ps[:, c * P:(c + 1) * P],
+                                cols[:, CHUNKS + c:CHUNKS + c + 1].to_broadcast([P, P]), ident[:])
+        neg_sg = sb.tile([P, I], F32, name="neg_sg")
+        nc.scalar.activation(out=neg_sg[:], in_=sg_ps[:, 0:I], func=ACT.Copy, scale=-1.0)
+
+        kp = sb.tile([P, I, PACK], BF16, name="kp", align_bytes=64)
+        slope = []
+        vp = []
+        for j in range(PACK):
+            picked = sb.tile([P, I], F32, name=f"picked{j}")
+            nc.vector.tensor_copy(picked[:], lift_sb[j][:].indirect(offs2_sb[:]))
+            l1 = sb.tile([P, I], F32, name=f"l1_{j}")
+            nc.scalar.activation(out=l1[:], in_=picked[:], func=ACT.Exp)
+            if j == 0:
+                scale_list = sb.tile([P, Q], U8, name="scale_list", align_bytes=64)
+                nc.vector.tensor_copy(scale_list[:], scale_pool[:].indirect(offs4_sb[:]))
+                q_scales = sb.tile([P, PACK, P], U8, name="q_scales", align_bytes=64)
+                nc.vector.tensor_copy(out=q_scales[:], in_=scale_list[:].rearrange("p (s r) -> p r s", r=PACK))
+            x1 = sb.tile([P, I], F32, name=f"x1_{j}")
+            nc.vector.tensor_tensor(x1[:], keys_sb[j][:].indirect(offs_sb[:]), l1[:], ALU.mult)
+            vp.append(sb.tile([P, I], F32, name=f"vp{j}"))
+            nc.scalar.activation(out=vp[j][:], in_=x1[:], func=ACT.Tanh)
+            nc.scalar.activation(out=kp[:, :, j], in_=vp[j][:], func=ACT.Copy, scale=ksc_sb[:, j:j + 1])
+        q_words = sb.tile([P, PACK, P], U32, name="q_words", align_bytes=64)
+        nc.vector.tensor_copy(q_words[:].rearrange("p r s -> p s r"), word_pool[:].indirect(offs4_sb[:]))
+        kp_words = sb.tile([P, I], U32, name="kp_words", align_bytes=64)
+        kp_scales = sb.tile([P, I], U8, name="kp_scales", align_bytes=64)
+        nc.vector.quantize_mx(out=kp_words[:].bitcast(FP8X4), scales=kp_scales[:],
+                              in_=kp[:].rearrange("p i j -> p (i j)"))
+
+        scores = [psum.tile([P, 2, I], F32, name=f"scores{b}", tag="score", bufs=4) for b in range(2)]
+        for r in range(PACK):
+            nc.tensor.matmul_mx(out=scores[r // 2][:, r % 2, :], lhsT=q_words[:, r, :].bitcast(FP8X4),
+                                lhsT_scale=q_scales[:, r, :], rhs=kp_words[:].bitcast(FP8X4),
+                                rhs_scale=kp_scales[:], start=True, stop=True)
+        tq = sb.tile([P, PACK, I], F32, name="tq")
+        for r in range(PACK):
+            nc.scalar.activation(out=tq[:, r, :], in_=target_sb[:, r, :], func=ACT.Copy, scale=qs_sb[:, r:r + 1])
+        ds = sb.tile([P, PACK, I], BF16, name="ds", align_bytes=64)
+        for b in range(2):
+            neg_max = sb.tile([P, 2], F32, name=f"neg_max{b}")
+            nc.vector.tensor_reduce(out=neg_max[:], in_=scores[b][:], axis=AXIS_X, op=ALU.max, negate=True)
+            sums = sb.tile([P, 2], F32, name=f"sums{b}")
+            p = sb.tile([P, 2, I], F32, name=f"p{b}")
+            for k in range(2):
+                nc.scalar.activation(out=p[:, k, :], in_=scores[b][:, k, :], func=ACT.Exp,
+                                     bias=neg_max[:, k:k + 1], scale=1.0, accum_out=sums[:, k:k + 1])
+            inv = sb.tile([P, 2], F32, name=f"inv{b}")
+            nc.vector.reciprocal(out=inv[:], in_=sums[:])
+            gain = sb.tile([P, 2], F32, name=f"gain{b}")
+            nc.vector.tensor_tensor(gain[:], inv[:], qs_sb[:, 2 * b:2 * b + 2], ALU.mult)
+            for k in range(2):
+                nc.vector.scalar_tensor_tensor(out=ds[:, 2 * b + k, :], in0=p[:, k, :], scalar=gain[:, k:k + 1],
+                                               in1=tq[:, 2 * b + k, :], op0=ALU.mult, op1=ALU.subtract)
+        ds_woven = sb.tile([P, I, PACK], BF16, name="ds_woven", align_bytes=64)
+        nc.vector.tensor_copy(out=ds_woven[:].rearrange("p (c i) r -> p c r i", i=4),
+                              in_=ds[:].rearrange("p r (c i) -> p c r i", i=4))
+        ds_words = sb.tile([P, I], U32, name="ds_words", align_bytes=64)
+        ds_scales = sb.tile([P, I], U8, name="ds_scales", align_bytes=64)
+        nc.vector.quantize_mx(out=ds_words[:].bitcast(FP8X4), scales=ds_scales[:],
+                              in_=ds_woven[:].rearrange("p i r -> p (i r)"))
+
+        qr = sb.tile([P, PACK, P, PACK], BF16, name="qr", align_bytes=64)
+        for part in range(4):
+            m = slice(part * 32, (part + 1) * 32)
+            nc.scalar.copy(out=qr[:, :, m, :].rearrange("p j m r -> p m r j"),
+                           in_=qrows_sb[:].rearrange("p r (m j) -> p m r j", j=PACK)[:, m, :, :])
+        qr_words = sb.tile([P, PACK, P], U32, name="qr_words", align_bytes=64)
+        qr_scales = sb.tile([P, PACK, P], U8, name="qr_scales", align_bytes=64)
+        nc.vector.quantize_mx(out=qr_words[:].rearrange("p j m -> p (j m)").bitcast(FP8X4),
+                              scales=qr_scales[:].rearrange("p j m -> p (j m)"),
+                              in_=qr[:].rearrange("p j m r -> p (j m r)"))
+
+        for j in range(PACK):
+            sq = sb.tile([P, I], F32, name=f"sq{j}")
+            nc.scalar.activation(out=sq[:], in_=vp[j][:], func=ACT.Square)
+            slope.append(sb.tile([P, I], F32, name=f"slope{j}"))
+            nc.vector.scalar_tensor_tensor(out=slope[j][:], in0=sq[:], scalar=1.0, in1=neg_sg[:],
+                                           op0=ALU.subtract, op1=ALU.mult)
+
+        grads = [psum.tile([P, 2, I], F32, name=f"grads{b}", tag="grad", bufs=2) for b in range(2)]
+        for j in range(PACK):
+            nc.tensor.matmul_mx(out=grads[j // 2][:, j % 2, :], lhsT=qr_words[:, j, :].bitcast(FP8X4),
+                                lhsT_scale=qr_scales[:, j, :], rhs=ds_words[:].bitcast(FP8X4),
+                                rhs_scale=ds_scales[:], start=True, stop=True)
+        for j in range(PACK):
+            c0 = sb.tile([P, I], F32, name=f"c0_{j}")
+            nc.scalar.copy(out=c0[:], in_=grads[j // 2][:, j % 2, :])
+            nc.vector.tensor_tensor(gf[j][:].indirect(offs_sb[:]), c0[:], slope[j][:], ALU.mult)
+
+        out_planes = out.rearrange("(p j) t -> j p t", j=PACK)
+        for h in range(T // BANK):
+            faded = []
+            for k in range(BANK // P):
+                c = h * (BANK // P) + k
+                turned = psum.tile([P, PACK, P], F32, name="turned", tag="turned", bufs=2)
+                for j in range(PACK):
+                    nc.tensor.transpose(turned[:, j, :], old_sb[h][:, j, k * P:(k + 1) * P], ident[:])
+                faded.append(sb.tile([P, PACK, P], F32, name=f"faded{c}"))
+                nc.scalar.activation(out=faded[k][:], in_=turned[:], func=ACT.Copy, scale=cols[:, c:c + 1])
+            for j in range(PACK):
+                back = psum.tile([P, BANK], F32, name="back", tag="score", bufs=4)
+                for k in range(BANK // P):
+                    nc.tensor.transpose(back[:, k * P:(k + 1) * P], faded[k][:, j, :], ident[:])
+                res = sb.tile([P, BANK], F32, name=f"res{h}_{j}")
+                nc.vector.tensor_tensor(res[:], back[:], gf[j][:, h * BANK:(h + 1) * BANK], ALU.add)
+                nc.sync.dma_start(out=out_planes[j][:, h * BANK:(h + 1) * BANK], in_=res[:])

@@ -39,37 +39,44 @@ def tile_attend_bklifted_s_kernel(tc, keys, qpool_words, qpool_scales, ksc, qs, 
         nc.gpsimd.memset(scale_pool[:].bitcast(I32), 0)
         rows = sb.tile([P, P], F32, name="rows")
         nc.gpsimd.memset(rows[:], 0.0)
-        ident = sb.tile([P, P], F32, name="ident")
-        make_identity(nc, ident[:])
         gf = [sb.tile([P, T], F32, name=f"gf{j}") for j in range(PACK)]
         for j in range(PACK):
-            nc.vector.memset(gf[j][:], 0.0)
+            (nc.vector if j < 2 else nc.gpsimd).memset(gf[j][:], 0.0)
+        ident = sb.tile([P, P], F32, name="ident")
+        make_identity(nc, ident[:])
 
         lift_planes = lift.rearrange("(p j) t -> j p t", j=PACK)
         keys_planes = keys.rearrange("(p j) t -> j p t", j=PACK)
         lift_sb = [sb.tile([P, T], F32, name=f"lift{j}") for j in range(PACK)]
-        keys_sb = [sb.tile([P, T], F32, name=f"keys{j}") for j in range(PACK)]
+        keys_sb = [sb.tile([P, T], F32, name=f"keys{j}", align_bytes=64) for j in range(PACK)]
         ksc_sb = sb.tile([P, PACK], F32, name="ksc_sb")
         qs_sb = sb.tile([P, PACK], F32, name="qs_sb")
-        nc.sync.dma_start(out=lift_sb[0][:], in_=lift_planes[0])
-        nc.sync.dma_start(offs2_sb[:], offs2)
-        nc.sync.dma_start(offs4_sb[:], offs4)
-        for quad in range(4):
+        def load_scale_rows(quad):
             nc.sync.dma_start(out=scale_pool[32 * quad:32 * quad + 4, :].bitcast(I32),
                               in_=qpool_scales[0][4 * quad:4 * quad + 4, :].bitcast(I32))
-        nc.sync.dma_start(out=keys_sb[0][:], in_=keys_planes[0])
+
+        nc.sync.dma_start(offs2_sb[:], offs2)
         nc.sync.dma_start(offs_sb[:], offs)
         nc.sync.dma_start(out=ksc_sb[:], in_=ksc.rearrange("(p j) o -> p (j o)", j=PACK))
-        for j in range(1, PACK):
+        nc.sync.dma_start(out=lift_sb[0][:], in_=lift_planes[0])
+        nc.sync.dma_start(out=keys_sb[0][:], in_=keys_planes[0])
+        nc.sync.dma_start(offs4_sb[:], offs4)
+        load_scale_rows(0)
+        load_scale_rows(1)
+        nc.sync.dma_start(out=lift_sb[1][:], in_=lift_planes[1])
+        load_scale_rows(2)
+        load_scale_rows(3)
+        nc.sync.dma_start(out=keys_sb[1][:], in_=keys_planes[1])
+        for j in range(2, PACK):
             nc.sync.dma_start(out=lift_sb[j][:], in_=lift_planes[j])
+        nc.sync.dma_start(out=rows[0:CHUNKS, :], in_=fade.rearrange("o (c p) -> (o c) p", p=P))
+        nc.sync.dma_start(out=rows[CHUNKS:CHUNKS + I // P, :], in_=sg.rearrange("o (c p) -> (o c) p", p=P))
+        nc.sync.dma_start(out=qs_sb[:], in_=qs.rearrange("(p r) o -> p (r o)", r=PACK))
+        for j in range(2, PACK):
             nc.sync.dma_start(out=keys_sb[j][:], in_=keys_planes[j])
-            if j == 1:
-                nc.sync.dma_start(out=rows[0:CHUNKS, :], in_=fade.rearrange("o (c p) -> (o c) p", p=P))
-                nc.sync.dma_start(out=rows[CHUNKS:CHUNKS + I // P, :], in_=sg.rearrange("o (c p) -> (o c) p", p=P))
         word_pool = sb.tile([P, U], U32, name="word_pool", align_bytes=64)
         nc.sync.dma_start(out=word_pool[:].bitcast(I32),
                           in_=qpool_words[0].rearrange("p u r -> p (u r)").bitcast(I32))
-        nc.sync.dma_start(out=qs_sb[:], in_=qs.rearrange("(p r) o -> p (r o)", r=PACK))
         target_sb = sb.tile([P, PACK, I], F32, name="target_sb")
         nc.sync.dma_start(out=target_sb[:], in_=target.rearrange("(p r) i -> p r i", r=PACK))
         qrows_sb = sb.tile([P, PACK, D], F32, name="qrows_sb")
@@ -79,6 +86,46 @@ def tile_attend_bklifted_s_kernel(tc, keys, qpool_words, qpool_scales, ksc, qs, 
         for h in range(T // BANK):
             nc.sync.dma_start(out=old_sb[h][:], in_=old_rows[:, :, h * BANK:(h + 1) * BANK])
 
+        kp_pairs = sb.tile([P, 2, I, 2], BF16, name="kp_pairs", align_bytes=64)
+        slope = []
+        vp = [sb.tile([P, 2, I], F32, name=f"vp{b}") for b in range(2)]
+        l1 = []
+
+        def lifted(j):
+            picked = sb.tile([P, I], F32, name=f"picked{j}")
+            nc.vector.tensor_copy(picked[:], lift_sb[j][:].indirect(offs2_sb[:]))
+            l1.append(sb.tile([P, I], F32, name=f"l1_{j}"))
+            nc.scalar.activation(out=l1[j][:], in_=picked[:], func=ACT.Exp)
+
+        def prepared(j):
+            x1 = sb.tile([P, I], F32, name=f"x1_{j}")
+            nc.vector.tensor_tensor(x1[:], keys_sb[j][:].indirect(offs_sb[:]), l1[j][:], ALU.mult)
+            nc.scalar.activation(out=vp[j // 2][:, j % 2, :], in_=x1[:], func=ACT.Tanh)
+            nc.scalar.activation(out=kp_pairs[:, j // 2, :, j % 2], in_=vp[j // 2][:, j % 2, :], func=ACT.Copy,
+                                 scale=ksc_sb[:, j:j + 1])
+
+        lifted(0)
+        prepared(0)
+        lifted(1)
+        scale_list = sb.tile([P, Q], U8, name="scale_list", align_bytes=64)
+        nc.vector.tensor_copy(scale_list[:], scale_pool[:].indirect(offs4_sb[:]))
+        prepared(1)
+        q_scales = sb.tile([P, PACK, P], U8, name="q_scales", align_bytes=64)
+        nc.vector.tensor_copy(out=q_scales[:], in_=scale_list[:].rearrange("p (s r) -> p r s", r=PACK))
+        lifted(2)
+        lifted(3)
+        prepared(2)
+        prepared(3)
+        q_words = sb.tile([P, PACK, P], U32, name="q_words", tag="keys3", align_bytes=64)
+        nc.vector.tensor_copy(q_words[:].rearrange("p r s -> p s r"), word_pool[:].indirect(offs4_sb[:]))
+        kp = sb.tile([P, I, PACK], BF16, name="kp", align_bytes=64)
+        nc.vector.tensor_copy(out=kp[:].rearrange("p i j -> p (i j)").bitcast(I32).rearrange("p (i b) -> p i b", b=2),
+                              in_=kp_pairs[:].rearrange("p b i e -> p b (i e)").bitcast(I32).rearrange("p b i -> p i b"))
+        kp_words = sb.tile([P, I], U32, name="kp_words", align_bytes=64)
+        kp_scales = sb.tile([P, I], U8, name="kp_scales", align_bytes=64)
+        nc.vector.quantize_mx(out=kp_words[:].bitcast(FP8X4), scales=kp_scales[:],
+                              in_=kp[:].rearrange("p i j -> p (i j)"))
+
         cols_ps = psum.tile([P, BANK], F32, name="cols_ps", tag="score", bufs=4)
         nc.tensor.transpose(cols_ps[:, 0:P], rows[:], ident[:])
         cols = sb.tile([P, 16], F32, name="cols")
@@ -87,108 +134,98 @@ def tile_attend_bklifted_s_kernel(tc, keys, qpool_words, qpool_scales, ksc, qs, 
         for c in range(I // P):
             nc.tensor.transpose(sg_ps[:, c * P:(c + 1) * P],
                                 cols[:, CHUNKS + c:CHUNKS + c + 1].to_broadcast([P, P]), ident[:])
-        neg_sg = sb.tile([P, I], F32, name="neg_sg")
+        neg_sg = sb.tile([P, I], F32, name="neg_sg", tag="l1_3")
         nc.scalar.activation(out=neg_sg[:], in_=sg_ps[:, 0:I], func=ACT.Copy, scale=-1.0)
 
-        kp = sb.tile([P, I, PACK], BF16, name="kp", align_bytes=64)
-        slope = []
-        vp = []
-        for j in range(PACK):
-            picked = sb.tile([P, I], F32, name=f"picked{j}")
-            nc.vector.tensor_copy(picked[:], lift_sb[j][:].indirect(offs2_sb[:]))
-            l1 = sb.tile([P, I], F32, name=f"l1_{j}")
-            nc.scalar.activation(out=l1[:], in_=picked[:], func=ACT.Exp)
-            if j == 0:
-                scale_list = sb.tile([P, Q], U8, name="scale_list", align_bytes=64)
-                nc.vector.tensor_copy(scale_list[:], scale_pool[:].indirect(offs4_sb[:]))
-                q_scales = sb.tile([P, PACK, P], U8, name="q_scales", align_bytes=64)
-                nc.vector.tensor_copy(out=q_scales[:], in_=scale_list[:].rearrange("p (s r) -> p r s", r=PACK))
-            x1 = sb.tile([P, I], F32, name=f"x1_{j}")
-            nc.vector.tensor_tensor(x1[:], keys_sb[j][:].indirect(offs_sb[:]), l1[:], ALU.mult)
-            vp.append(sb.tile([P, I], F32, name=f"vp{j}"))
-            nc.scalar.activation(out=vp[j][:], in_=x1[:], func=ACT.Tanh)
-            nc.scalar.activation(out=kp[:, :, j], in_=vp[j][:], func=ACT.Copy, scale=ksc_sb[:, j:j + 1])
-        q_words = sb.tile([P, PACK, P], U32, name="q_words", align_bytes=64)
-        nc.vector.tensor_copy(q_words[:].rearrange("p r s -> p s r"), word_pool[:].indirect(offs4_sb[:]))
-        kp_words = sb.tile([P, I], U32, name="kp_words", align_bytes=64)
-        kp_scales = sb.tile([P, I], U8, name="kp_scales", align_bytes=64)
-        nc.vector.quantize_mx(out=kp_words[:].bitcast(FP8X4), scales=kp_scales[:],
-                              in_=kp[:].rearrange("p i j -> p (i j)"))
-
-        scores = [psum.tile([P, 2, I], F32, name=f"scores{b}", tag="score", bufs=4) for b in range(2)]
+        scores = [psum.tile([P, I], F32, name=f"scores{r}", tag="score", bufs=4) for r in range(PACK)]
         for r in range(PACK):
-            nc.tensor.matmul_mx(out=scores[r // 2][:, r % 2, :], lhsT=q_words[:, r, :].bitcast(FP8X4),
+            nc.tensor.matmul_mx(out=scores[r][:], lhsT=q_words[:, r, :].bitcast(FP8X4),
                                 lhsT_scale=q_scales[:, r, :], rhs=kp_words[:].bitcast(FP8X4),
                                 rhs_scale=kp_scales[:], start=True, stop=True)
         tq = sb.tile([P, PACK, I], F32, name="tq")
         for r in range(PACK):
             nc.scalar.activation(out=tq[:, r, :], in_=target_sb[:, r, :], func=ACT.Copy, scale=qs_sb[:, r:r + 1])
         ds = sb.tile([P, PACK, I], BF16, name="ds", align_bytes=64)
-        for b in range(2):
-            neg_max = sb.tile([P, 2], F32, name=f"neg_max{b}")
-            nc.vector.tensor_reduce(out=neg_max[:], in_=scores[b][:], axis=AXIS_X, op=ALU.max, negate=True)
-            sums = sb.tile([P, 2], F32, name=f"sums{b}")
-            p = sb.tile([P, 2, I], F32, name=f"p{b}")
-            for k in range(2):
-                nc.scalar.activation(out=p[:, k, :], in_=scores[b][:, k, :], func=ACT.Exp,
-                                     bias=neg_max[:, k:k + 1], scale=1.0, accum_out=sums[:, k:k + 1])
-            inv = sb.tile([P, 2], F32, name=f"inv{b}")
+        for group in ((0, 1), (2,), (3,)):
+            first, count = group[0], len(group)
+            sums = sb.tile([P, count], F32, name=f"sums{first}")
+            p = sb.tile([P, count, I], F32, name=f"p{first}")
+            for k, r in enumerate(group):
+                neg_max = sb.tile([P, 1], F32, name=f"neg_max{r}", align_bytes=64)
+                nc.vector.tensor_reduce(out=neg_max[:], in_=scores[r][:], axis=AXIS_X, op=ALU.max, negate=True)
+                nc.scalar.activation(out=p[:, k, :], in_=scores[r][:], func=ACT.Exp,
+                                     bias=neg_max[:], scale=1.0, accum_out=sums[:, k:k + 1])
+            inv = sb.tile([P, count], F32, name=f"inv{first}")
             nc.vector.reciprocal(out=inv[:], in_=sums[:])
-            gain = sb.tile([P, 2], F32, name=f"gain{b}")
-            nc.vector.tensor_tensor(gain[:], inv[:], qs_sb[:, 2 * b:2 * b + 2], ALU.mult)
-            for k in range(2):
-                nc.vector.scalar_tensor_tensor(out=ds[:, 2 * b + k, :], in0=p[:, k, :], scalar=gain[:, k:k + 1],
-                                               in1=tq[:, 2 * b + k, :], op0=ALU.mult, op1=ALU.subtract)
-        ds_woven = sb.tile([P, I, PACK], BF16, name="ds_woven", align_bytes=64)
-        nc.vector.tensor_copy(out=ds_woven[:].rearrange("p (c i) r -> p c r i", i=4),
-                              in_=ds[:].rearrange("p r (c i) -> p c r i", i=4))
+            gain = sb.tile([P, count], F32, name=f"gain{first}")
+            nc.vector.tensor_tensor(gain[:], inv[:], qs_sb[:, first:first + count], ALU.mult)
+            for k, r in enumerate(group):
+                nc.vector.scalar_tensor_tensor(out=ds[:, r, :], in0=p[:, k, :], scalar=gain[:, k:k + 1],
+                                               in1=tq[:, r, :], op0=ALU.mult, op1=ALU.subtract)
+        ds_woven = [sb.tile([P, I // 2, PACK], BF16, name=f"ds_woven{a}", align_bytes=64) for a in range(2)]
         ds_words = sb.tile([P, I], U32, name="ds_words", align_bytes=64)
         ds_scales = sb.tile([P, I], U8, name="ds_scales", align_bytes=64)
-        nc.vector.quantize_mx(out=ds_words[:].bitcast(FP8X4), scales=ds_scales[:],
-                              in_=ds_woven[:].rearrange("p i r -> p (i r)"))
+        halves = [slice(0, I // 2), slice(I // 2, I)]
+        for a, half in enumerate(halves):
+            nc.vector.tensor_copy(out=ds_woven[a][:].rearrange("p (c i) r -> p c r i", i=4),
+                                  in_=ds[:, :, half].rearrange("p r (c i) -> p c r i", i=4))
+        for a, half in enumerate(halves):
+            nc.vector.quantize_mx(out=ds_words[:, half].bitcast(FP8X4), scales=ds_scales[:, half],
+                                  in_=ds_woven[a][:].rearrange("p i r -> p (i r)"))
 
-        qr = sb.tile([P, PACK, P, PACK], BF16, name="qr", align_bytes=64)
-        for part in range(4):
-            m = slice(part * 32, (part + 1) * 32)
-            nc.scalar.copy(out=qr[:, :, m, :].rearrange("p j m r -> p m r j"),
-                           in_=qrows_sb[:].rearrange("p r (m j) -> p m r j", j=PACK)[:, m, :, :])
-        qr_words = sb.tile([P, PACK, P], U32, name="qr_words", align_bytes=64)
-        qr_scales = sb.tile([P, PACK, P], U8, name="qr_scales", align_bytes=64)
-        nc.vector.quantize_mx(out=qr_words[:].rearrange("p j m -> p (j m)").bitcast(FP8X4),
-                              scales=qr_scales[:].rearrange("p j m -> p (j m)"),
-                              in_=qr[:].rearrange("p j m r -> p (j m r)"))
+        qr = sb.tile([P, PACK, P, PACK], BF16, name="qr", tag="neg_max3", align_bytes=64)
+        qr_words = [sb.tile([P, 2, P], U32, name=f"qr_words{b}", tag=("qr_words0", "ds_woven0")[b], align_bytes=64)
+                    for b in range(2)]
+        qr_scales = [sb.tile([P, 2, P], U8, name=f"qr_scales{b}", align_bytes=64) for b in range(2)]
+        for b in range(2):
+            pair = slice(2 * b, 2 * b + 2)
+            nc.scalar.copy(out=qr[:, pair, :, :].rearrange("p j m r -> p m r j"),
+                           in_=qrows_sb[:].rearrange("p r (m j) -> p m r j", j=PACK)[:, :, :, pair])
+            nc.vector.quantize_mx(out=qr_words[b][:].rearrange("p j m -> p (j m)").bitcast(FP8X4),
+                                  scales=qr_scales[b][:].rearrange("p j m -> p (j m)"),
+                                  in_=qr[:, pair, :, :].rearrange("p j m r -> p (j m r)"))
 
-        for j in range(PACK):
-            sq = sb.tile([P, I], F32, name=f"sq{j}")
-            nc.scalar.activation(out=sq[:], in_=vp[j][:], func=ACT.Square)
-            slope.append(sb.tile([P, I], F32, name=f"slope{j}"))
-            nc.vector.scalar_tensor_tensor(out=slope[j][:], in0=sq[:], scalar=1.0, in1=neg_sg[:],
+        for first, count, sq_tag, slope_tag in ((0, 2, "picked3", "kp"), (2, 2, "x1_3", "ds_woven1")):
+            part = slice(first % 2, first % 2 + count)
+            sq = sb.tile([P, count, I], F32, name=f"sq{first}", tag=sq_tag)
+            nc.scalar.activation(out=sq[:], in_=vp[first // 2][:, part, :], func=ACT.Square)
+            made = sb.tile([P, count, I], F32, name=f"slope{first}", tag=slope_tag, align_bytes=64)
+            nc.vector.scalar_tensor_tensor(out=made[:], in0=sq[:], scalar=1.0,
+                                           in1=neg_sg[:].unsqueeze(1).to_broadcast([P, count, I]),
                                            op0=ALU.subtract, op1=ALU.mult)
+            slope.extend(made[:, k, :] for k in range(count))
 
-        grads = [psum.tile([P, 2, I], F32, name=f"grads{b}", tag="grad", bufs=2) for b in range(2)]
-        for j in range(PACK):
-            nc.tensor.matmul_mx(out=grads[j // 2][:, j % 2, :], lhsT=qr_words[:, j, :].bitcast(FP8X4),
-                                lhsT_scale=qr_scales[:, j, :], rhs=ds_words[:].bitcast(FP8X4),
-                                rhs_scale=ds_scales[:], start=True, stop=True)
-        for j in range(PACK):
-            c0 = sb.tile([P, I], F32, name=f"c0_{j}")
-            nc.scalar.copy(out=c0[:], in_=grads[j // 2][:, j % 2, :])
-            nc.vector.tensor_tensor(gf[j][:].indirect(offs_sb[:]), c0[:], slope[j][:], ALU.mult)
+        banks = [[(0, halves[0])], [(0, halves[1]), (1, slice(0, I))], [(2, slice(0, I)), (3, slice(0, I))]]
+        for b, pieces in enumerate(banks):
+            grads = psum.tile([P, 2, I], F32, name=f"grads{b}", tag="back", bufs=4)
+            for k, (j, part) in enumerate(pieces):
+                nc.tensor.matmul_mx(out=grads[:, k, part], lhsT=qr_words[j // 2][:, j % 2, :].bitcast(FP8X4),
+                                    lhsT_scale=qr_scales[j // 2][:, j % 2, :], rhs=ds_words[:, part].bitcast(FP8X4),
+                                    rhs_scale=ds_scales[:, part], start=True, stop=True)
+            for k, (j, part) in enumerate(pieces):
+                c0 = sb.tile([P, part.stop - part.start], F32, name=f"c0_{b}_{k}")
+                nc.scalar.copy(out=c0[:], in_=grads[:, k, part])
+                nc.vector.tensor_tensor(gf[j][:].indirect(offs_sb[:, part.start // 16:part.stop // 16]), c0[:],
+                                        slope[j][:, part], ALU.mult)
 
+        held_back = {2: "qr_words0", 3: "ds_words", 4: "qr_scales1", 5: "ds_scales"}
         out_planes = out.rearrange("(p j) t -> j p t", j=PACK)
         for h in range(T // BANK):
             faded = []
             for k in range(BANK // P):
                 c = h * (BANK // P) + k
-                turned = psum.tile([P, PACK, P], F32, name="turned", tag="turned", bufs=2)
+                turned = psum.tile([P, PACK, P], F32, name="turned", tag="score", bufs=4)
                 for j in range(PACK):
                     nc.tensor.transpose(turned[:, j, :], old_sb[h][:, j, k * P:(k + 1) * P], ident[:])
-                faded.append(sb.tile([P, PACK, P], F32, name=f"faded{c}"))
+                faded.append(sb.tile([P, PACK, P], F32, name=f"faded{c}", tag=held_back.get(c, f"faded{c}"),
+                                     align_bytes=64))
                 nc.scalar.activation(out=faded[k][:], in_=turned[:], func=ACT.Copy, scale=cols[:, c:c + 1])
             for j in range(PACK):
-                back = psum.tile([P, BANK], F32, name="back", tag="score", bufs=4)
+                back = psum.tile([P, BANK], F32, name="back", tag="back", bufs=4)
                 for k in range(BANK // P):
                     nc.tensor.transpose(back[:, k * P:(k + 1) * P], faded[k][:, j, :], ident[:])
-                res = sb.tile([P, BANK], F32, name=f"res{h}_{j}")
-                nc.vector.tensor_tensor(res[:], back[:], gf[j][:, h * BANK:(h + 1) * BANK], ALU.add)
-                nc.sync.dma_start(out=out_planes[j][:, h * BANK:(h + 1) * BANK], in_=res[:])
+                last = h == T // BANK - 1 and j == PACK - 1
+                for lo, hi in ((0, 384), (384, BANK)) if last else ((0, BANK),):
+                    res = sb.tile([P, hi - lo], F32, name=f"res{h}_{j}_{lo}")
+                    nc.vector.tensor_tensor(res[:], back[:, lo:hi], gf[j][:, h * BANK + lo:h * BANK + hi], ALU.add)
+                    nc.sync.dma_start(out=out_planes[j][:, h * BANK + lo:h * BANK + hi], in_=res[:])

@@ -41,13 +41,13 @@ def tile_attend_bklifted_s_kernel(tc, keys, qpool_words, qpool_scales, ksc, qs, 
         nc.gpsimd.memset(rows[:], 0.0)
         gf = [sb.tile([P, T], F32, name=f"gf{j}") for j in range(PACK)]
         for j in range(PACK):
-            (nc.vector if j < 2 else nc.gpsimd).memset(gf[j][:], 0.0)
+            nc.vector.memset(gf[j][:], 0.0)
         ident = sb.tile([P, P], F32, name="ident")
         make_identity(nc, ident[:])
 
-        lift_planes = lift.rearrange("(p j) t -> j p t", j=PACK)
+        lift_rows = lift.rearrange("(p j) t -> p j t", j=PACK)
         keys_planes = keys.rearrange("(p j) t -> j p t", j=PACK)
-        lift_sb = [sb.tile([P, T], F32, name=f"lift{j}") for j in range(PACK)]
+        lift_sb = [sb.tile([P, 2, T], F32, name=f"lift{b}") for b in range(2)]
         keys_sb = [sb.tile([P, T], F32, name=f"keys{j}", align_bytes=64) for j in range(PACK)]
         ksc_sb = sb.tile([P, PACK], F32, name="ksc_sb")
         qs_sb = sb.tile([P, PACK], F32, name="qs_sb")
@@ -56,19 +56,17 @@ def tile_attend_bklifted_s_kernel(tc, keys, qpool_words, qpool_scales, ksc, qs, 
                               in_=qpool_scales[0][4 * quad:4 * quad + 4, :].bitcast(I32))
 
         nc.sync.dma_start(offs2_sb[:], offs2)
+        nc.sync.dma_start(out=lift_sb[0][:], in_=lift_rows[:, 0:2, :])
         nc.sync.dma_start(offs_sb[:], offs)
         nc.sync.dma_start(out=ksc_sb[:], in_=ksc.rearrange("(p j) o -> p (j o)", j=PACK))
-        nc.sync.dma_start(out=lift_sb[0][:], in_=lift_planes[0])
         nc.sync.dma_start(out=keys_sb[0][:], in_=keys_planes[0])
         nc.sync.dma_start(offs4_sb[:], offs4)
         load_scale_rows(0)
         load_scale_rows(1)
-        nc.sync.dma_start(out=lift_sb[1][:], in_=lift_planes[1])
+        nc.sync.dma_start(out=keys_sb[1][:], in_=keys_planes[1])
         load_scale_rows(2)
         load_scale_rows(3)
-        nc.sync.dma_start(out=keys_sb[1][:], in_=keys_planes[1])
-        for j in range(2, PACK):
-            nc.sync.dma_start(out=lift_sb[j][:], in_=lift_planes[j])
+        nc.sync.dma_start(out=lift_sb[1][:], in_=lift_rows[:, 2:4, :])
         nc.sync.dma_start(out=rows[0:CHUNKS, :], in_=fade.rearrange("o (c p) -> (o c) p", p=P))
         nc.sync.dma_start(out=rows[CHUNKS:CHUNKS + I // P, :], in_=sg.rearrange("o (c p) -> (o c) p", p=P))
         nc.sync.dma_start(out=qs_sb[:], in_=qs.rearrange("(p r) o -> p (r o)", r=PACK))
@@ -93,7 +91,7 @@ def tile_attend_bklifted_s_kernel(tc, keys, qpool_words, qpool_scales, ksc, qs, 
 
         def lifted(j):
             picked = sb.tile([P, I], F32, name=f"picked{j}")
-            nc.vector.tensor_copy(picked[:], lift_sb[j][:].indirect(offs2_sb[:]))
+            nc.vector.tensor_copy(picked[:], lift_sb[j // 2][:, j % 2, :].indirect(offs2_sb[:]))
             l1.append(sb.tile([P, I], F32, name=f"l1_{j}"))
             nc.scalar.activation(out=l1[j][:], in_=picked[:], func=ACT.Exp)
 
@@ -105,11 +103,11 @@ def tile_attend_bklifted_s_kernel(tc, keys, qpool_words, qpool_scales, ksc, qs, 
                                  scale=ksc_sb[:, j:j + 1])
 
         lifted(0)
-        prepared(0)
         lifted(1)
+        prepared(0)
+        prepared(1)
         scale_list = sb.tile([P, Q], U8, name="scale_list", align_bytes=64)
         nc.vector.tensor_copy(scale_list[:], scale_pool[:].indirect(offs4_sb[:]))
-        prepared(1)
         q_scales = sb.tile([P, PACK, P], U8, name="q_scales", align_bytes=64)
         nc.vector.tensor_copy(out=q_scales[:], in_=scale_list[:].rearrange("p (s r) -> p r s", r=PACK))
         lifted(2)
@@ -185,7 +183,7 @@ def tile_attend_bklifted_s_kernel(tc, keys, qpool_words, qpool_scales, ksc, qs, 
                                   scales=qr_scales[b][:].rearrange("p j m -> p (j m)"),
                                   in_=qr[:, pair, :, :].rearrange("p j m r -> p (j m r)"))
 
-        for first, count, sq_tag, slope_tag in ((0, 2, "picked3", "kp"), (2, 2, "x1_3", "ds_woven1")):
+        for first, count, sq_tag, slope_tag in ((0, 2, "sq0", "kp"), (2, 2, "x1_3", "ds_woven1")):
             part = slice(first % 2, first % 2 + count)
             sq = sb.tile([P, count, I], F32, name=f"sq{first}", tag=sq_tag)
             nc.scalar.activation(out=sq[:], in_=vp[first // 2][:, part, :], func=ACT.Square)

from contextlib import ExitStack

import concourse.mybir as mybir
from concourse.masks import make_identity

D, T, I, Q, U = 512, 1024, 256, 512, 1024
FLOPS = 2 * 2 * D * Q * I

F32 = mybir.dt.float32
BF16 = mybir.dt.bfloat16
I32 = mybir.dt.int32
U32 = mybir.dt.uint32
U16 = mybir.dt.uint16
U8 = mybir.dt.uint8
FP8X4 = mybir.dt.float8_e4m3fn_x4
ACT = mybir.ActivationFunctionType
ALU = mybir.AluOpType
AXIS_X = mybir.AxisListType.X

P = 128
PACK = 4
BANK = 512
CHUNKS = T // P


def tile_attend_bklifted_s_kernel(tc, keys, qpool_words, qpool_scales, ksc, qs, target, qrows, lift, sg, old, fade,
                                   offs, offs2, offs4, out):
    nc = tc.nc
    with ExitStack() as ctx:
        lists = ctx.enter_context(tc.tile_pool(name="lists", bufs=1))
        sb = ctx.enter_context(tc.tile_pool(name="sb", bufs=1))
        psum = ctx.enter_context(tc.psum_pool(name="psum", bufs=1))

        offs_sb = lists.tile([P, I // 16], U16, name="offs_sb")
        offs2_sb = lists.tile([P, I // 16], U16, name="offs2_sb")
        offs4_sb = lists.tile([P, Q // 16], U16, name="offs4_sb")

        scale_pool = sb.tile([P, U], U8, name="scale_pool", align_bytes=64)
        nc.gpsimd.memset(scale_pool[:].bitcast(I32), 0)
        rows = sb.tile([P, P], F32, name="rows")
        nc.gpsimd.memset(rows[:], 0.0)
        gf = [sb.tile([P, T], F32, name=f"gf{j}") for j in range(PACK)]
        for j in range(PACK):
            nc.vector.memset(gf[j][:], 0.0)
        ident = sb.tile([P, P], F32, name="ident")
        make_identity(nc, ident[:])

        lift_rows = lift.rearrange("(p j) t -> p j t", j=PACK)
        keys_planes = keys.rearrange("(p j) t -> j p t", j=PACK)
        lift_sb = [sb.tile([P, 2, T], F32, name=f"lift{b}") for b in range(2)]
        keys_sb = [sb.tile([P, T], F32, name=f"keys{j}", align_bytes=64) for j in range(PACK)]
        ksc_sb = sb.tile([P, PACK], F32, name="ksc_sb")
        qs_sb = sb.tile([P, PACK], F32, name="qs_sb")
        def load_scale_rows(quad):
            nc.sync.dma_start(out=scale_pool[32 * quad:32 * quad + 4, :].bitcast(I32),
                              in_=qpool_scales[0][4 * quad:4 * quad + 4, :].bitcast(I32))

        nc.sync.dma_start(offs2_sb[:], offs2)
        nc.sync.dma_start(out=lift_sb[0][:], in_=lift_rows[:, 0:2, :])
        nc.sync.dma_start(offs_sb[:], offs)
        nc.sync.dma_start(out=ksc_sb[:], in_=ksc.rearrange("(p j) o -> p (j o)", j=PACK))
        nc.sync.dma_start(out=keys_sb[0][:], in_=keys_planes[0])
        nc.sync.dma_start(offs4_sb[:], offs4)
        load_scale_rows(0)
        load_scale_rows(1)
        nc.sync.dma_start(out=keys_sb[1][:], in_=keys_planes[1])
        load_scale_rows(2)
        load_scale_rows(3)
        nc.sync.dma_start(out=lift_sb[1][:], in_=lift_rows[:, 2:4, :])
        nc.sync.dma_start(out=rows[0:CHUNKS, :], in_=fade.rearrange("o (c p) -> (o c) p", p=P))
        nc.sync.dma_start(out=rows[CHUNKS:CHUNKS + I // P, :], in_=sg.rearrange("o (c p) -> (o c) p", p=P))
        nc.sync.dma_start(out=qs_sb[:], in_=qs.rearrange("(p r) o -> p (r o)", r=PACK))
        for j in range(2, PACK):
            nc.sync.dma_start(out=keys_sb[j][:], in_=keys_planes[j])
        word_pool = sb.tile([P, U], U32, name="word_pool", align_bytes=64)
        nc.sync.dma_start(out=word_pool[:].bitcast(I32),
                          in_=qpool_words[0].rearrange("p u r -> p (u r)").bitcast(I32))
        target_sb = sb.tile([P, PACK, I], F32, name="target_sb")
        nc.sync.dma_start(out=target_sb[:], in_=target.rearrange("(p r) i -> p r i", r=PACK))
        qrows_sb = sb.tile([P, PACK, D], F32, name="qrows_sb")
        nc.sync.dma_start(out=qrows_sb[:], in_=qrows.rearrange("(p r) d -> p r d", r=PACK))
        old_rows = old.rearrange("(p j) t -> p j t", j=PACK)
        old_sb = [sb.tile([P, PACK, BANK], F32, name=f"old{h}") for h in range(T // BANK)]
        for h in range(T // BANK):
            nc.sync.dma_start(out=old_sb[h][:], in_=old_rows[:, :, h * BANK:(h + 1) * BANK])

        kp_pairs = sb.tile([P, 2, I, 2], BF16, name="kp_pairs", align_bytes=64)
        slope = []
        vp = [sb.tile([P, 2, I], F32, name=f"vp{b}") for b in range(2)]
        l1 = []

        def lifted(j):
            picked = sb.tile([P, I], F32, name=f"picked{j}")
            nc.vector.tensor_copy(picked[:], lift_sb[j // 2][:, j % 2, :].indirect(offs2_sb[:]))
            l1.append(sb.tile([P, I], F32, name=f"l1_{j}"))
            nc.scalar.activation(out=l1[j][:], in_=picked[:], func=ACT.Exp)

        def prepared(j):
            x1 = sb.tile([P, I], F32, name=f"x1_{j}")
            nc.vector.tensor_tensor(x1[:], keys_sb[j][:].indirect(offs_sb[:]), l1[j][:], ALU.mult)
            nc.scalar.activation(out=vp[j // 2][:, j % 2, :], in_=x1[:], func=ACT.Tanh)
            nc.scalar.activation(out=kp_pairs[:, j // 2, :, j % 2], in_=vp[j // 2][:, j % 2, :], func=ACT.Copy,
                                 scale=ksc_sb[:, j:j + 1])

        lifted(0)
        lifted(1)
        prepared(0)
        prepared(1)
        scale_list = sb.tile([P, Q], U8, name="scale_list", align_bytes=64)
        nc.vector.tensor_copy(scale_list[:], scale_pool[:].indirect(offs4_sb[:]))
        q_scales = sb.tile([P, PACK, P], U8, name="q_scales", align_bytes=64)
        nc.vector.tensor_copy(out=q_scales[:], in_=scale_list[:].rearrange("p (s r) -> p r s", r=PACK))
        lifted(2)
        lifted(3)
        prepared(2)
        prepared(3)
        q_words = sb.tile([P, PACK, P], U32, name="q_words", tag="keys3", align_bytes=64)
        nc.vector.tensor_copy(q_words[:].rearrange("p r s -> p s r"), word_pool[:].indirect(offs4_sb[:]))
        kp = sb.tile([P, I, PACK], BF16, name="kp", align_bytes=64)
        nc.vector.tensor_copy(out=kp[:].rearrange("p i j -> p (i j)").bitcast(I32).rearrange("p (i b) -> p i b", b=2),
                              in_=kp_pairs[:].rearrange("p b i e -> p b (i e)").bitcast(I32).rearrange("p b i -> p i b"))
        kp_words = sb.tile([P, I], U32, name="kp_words", align_bytes=64)
        kp_scales = sb.tile([P, I], U8, name="kp_scales", align_bytes=64)
        nc.vector.quantize_mx(out=kp_words[:].bitcast(FP8X4), scales=kp_scales[:],
                              in_=kp[:].rearrange("p i j -> p (i j)"))

        cols_ps = psum.tile([P, BANK], F32, name="cols_ps", tag="score", bufs=4)
        nc.tensor.transpose(cols_ps[:, 0:P], rows[:], ident[:])
        cols = sb.tile([P, 16], F32, name="cols")
        nc.scalar.copy(out=cols[:], in_=cols_ps[:, 0:16])
        sg_ps = psum.tile([P, BANK], F32, name="sg_ps", tag="score", bufs=4)
        for c in range(I // P):
            nc.tensor.transpose(sg_ps[:, c * P:(c + 1) * P],
                                cols[:, CHUNKS + c:CHUNKS + c + 1].to_broadcast([P, P]), ident[:])
        neg_sg = sb.tile([P, I], F32, name="neg_sg", tag="l1_3")
        nc.scalar.activation(out=neg_sg[:], in_=sg_ps[:, 0:I], func=ACT.Copy, scale=-1.0)

        scores = [psum.tile([P, I], F32, name=f"scores{r}", tag="score", bufs=4) for r in range(PACK)]
        for r in range(PACK):
            nc.tensor.matmul_mx(out=scores[r][:], lhsT=q_words[:, r, :].bitcast(FP8X4),
                                lhsT_scale=q_scales[:, r, :], rhs=kp_words[:].bitcast(FP8X4),
                                rhs_scale=kp_scales[:], start=True, stop=True)
        tq = sb.tile([P, PACK, I], F32, name="tq")
        for r in range(PACK):
            nc.scalar.activation(out=tq[:, r, :], in_=target_sb[:, r, :], func=ACT.Copy, scale=qs_sb[:, r:r + 1])
        ds = sb.tile([P, PACK, I], BF16, name="ds", align_bytes=64)
        for group in ((0, 1), (2,), (3,)):
            first, count = group[0], len(group)
            sums = sb.tile([P, count], F32, name=f"sums{first}")
            p = sb.tile([P, count, I], F32, name=f"p{first}")
            for k, r in enumerate(group):
                neg_max = sb.tile([P, 1], F32, name=f"neg_max{r}", align_bytes=64)
                nc.vector.tensor_reduce(out=neg_max[:], in_=scores[r][:], axis=AXIS_X, op=ALU.max, negate=True)
                nc.scalar.activation(out=p[:, k, :], in_=scores[r][:], func=ACT.Exp,
                                     bias=neg_max[:], scale=1.0, accum_out=sums[:, k:k + 1])
            inv = sb.tile([P, count], F32, name=f"inv{first}")
            nc.vector.reciprocal(out=inv[:], in_=sums[:])
            gain = sb.tile([P, count], F32, name=f"gain{first}")
            nc.vector.tensor_tensor(gain[:], inv[:], qs_sb[:, first:first + count], ALU.mult)
            for k, r in enumerate(group):
                nc.vector.scalar_tensor_tensor(out=ds[:, r, :], in0=p[:, k, :], scalar=gain[:, k:k + 1],
                                               in1=tq[:, r, :], op0=ALU.mult, op1=ALU.subtract)
        ds_woven = [sb.tile([P, I // 2, PACK], BF16, name=f"ds_woven{a}", align_bytes=64) for a in range(2)]
        ds_words = sb.tile([P, I], U32, name="ds_words", align_bytes=64)
        ds_scales = sb.tile([P, I], U8, name="ds_scales", align_bytes=64)
        halves = [slice(0, I // 2), slice(I // 2, I)]
        for a, half in enumerate(halves):
            nc.vector.tensor_copy(out=ds_woven[a][:].rearrange("p (c i) r -> p c r i", i=4),
                                  in_=ds[:, :, half].rearrange("p r (c i) -> p c r i", i=4))
        for a, half in enumerate(halves):
            nc.vector.quantize_mx(out=ds_words[:, half].bitcast(FP8X4), scales=ds_scales[:, half],
                                  in_=ds_woven[a][:].rearrange("p i r -> p (i r)"))

        qr = sb.tile([P, PACK, P, PACK], BF16, name="qr", tag="neg_max3", align_bytes=64)
        qr_words = [sb.tile([P, 2, P], U32, name=f"qr_words{b}", tag=("qr_words0", "ds_woven0")[b], align_bytes=64)
                    for b in range(2)]
        qr_scales = [sb.tile([P, 2, P], U8, name=f"qr_scales{b}", align_bytes=64) for b in range(2)]
        for b in range(2):
            pair = slice(2 * b, 2 * b + 2)
            nc.scalar.copy(out=qr[:, pair, :, :].rearrange("p j m r -> p m r j"),
                           in_=qrows_sb[:].rearrange("p r (m j) -> p m r j", j=PACK)[:, :, :, pair])
            nc.vector.quantize_mx(out=qr_words[b][:].rearrange("p j m -> p (j m)").bitcast(FP8X4),
                                  scales=qr_scales[b][:].rearrange("p j m -> p (j m)"),
                                  in_=qr[:, pair, :, :].rearrange("p j m r -> p (j m r)"))

        for first, count, sq_tag, slope_tag in ((0, 2, "sq0", "kp"), (2, 2, "x1_3", "ds_woven1")):
            part = slice(first % 2, first % 2 + count)
            sq = sb.tile([P, count, I], F32, name=f"sq{first}", tag=sq_tag)
            nc.scalar.activation(out=sq[:], in_=vp[first // 2][:, part, :], func=ACT.Square)
            made = sb.tile([P, count, I], F32, name=f"slope{first}", tag=slope_tag, align_bytes=64)
            nc.vector.scalar_tensor_tensor(out=made[:], in0=sq[:], scalar=1.0,
                                           in1=neg_sg[:].unsqueeze(1).to_broadcast([P, count, I]),
                                           op0=ALU.subtract, op1=ALU.mult)
            slope.extend(made[:, k, :] for k in range(count))

        banks = [[(0, halves[0])], [(0, halves[1]), (1, slice(0, I))], [(2, slice(0, I)), (3, slice(0, I))]]
        for b, pieces in enumerate(banks):
            grads = psum.tile([P, 2, I], F32, name=f"grads{b}", tag="back", bufs=4)
            for k, (j, part) in enumerate(pieces):
                nc.tensor.matmul_mx(out=grads[:, k, part], lhsT=qr_words[j // 2][:, j % 2, :].bitcast(FP8X4),
                                    lhsT_scale=qr_scales[j // 2][:, j % 2, :], rhs=ds_words[:, part].bitcast(FP8X4),
                                    rhs_scale=ds_scales[:, part], start=True, stop=True)
            for k, (j, part) in enumerate(pieces):
                c0 = sb.tile([P, part.stop - part.start], F32, name=f"c0_{b}_{k}")
                nc.scalar.copy(out=c0[:], in_=grads[:, k, part])
                nc.vector.tensor_tensor(gf[j][:].indirect(offs_sb[:, part.start // 16:part.stop // 16]), c0[:],
                                        slope[j][:, part], ALU.mult)

        held_back = {2: "qr_words0", 3: "ds_words", 4: "qr_scales1", 5: "ds_scales"}
        out_planes = out.rearrange("(p j) t -> j p t", j=PACK)
        for h in range(T // BANK):
            faded = []
            for k in range(BANK // P):
                c = h * (BANK // P) + k
                turned = psum.tile([P, PACK, P], F32, name="turned", tag="score", bufs=4)
                for j in range(PACK):
                    nc.tensor.transpose(turned[:, j, :], old_sb[h][:, j, k * P:(k + 1) * P], ident[:])
                faded.append(sb.tile([P, PACK, P], F32, name=f"faded{c}", tag=held_back.get(c, f"faded{c}"),
                                     align_bytes=64))
                nc.scalar.activation(out=faded[k][:], in_=turned[:], func=ACT.Copy, scale=cols[:, c:c + 1])
            for j in range(PACK):
                back = psum.tile([P, BANK], F32, name="back", tag="back", bufs=4)
                for k in range(BANK // P):
                    nc.tensor.transpose(back[:, k * P:(k + 1) * P], faded[k][:, j, :], ident[:])
                last = h == T // BANK - 1 and j == PACK - 1
                for lo, hi in ((0, 384), (384, BANK)) if last else ((0, BANK),):
                    res = sb.tile([P, hi - lo], F32, name=f"res{h}_{j}_{lo}")
                    nc.vector.tensor_tensor(res[:], back[:, lo:hi], gf[j][:, h * BANK + lo:h * BANK + hi], ALU.add)
                    nc.sync.dma_start(out=out_planes[j][:, h * BANK + lo:h * BANK + hi], in_=res[:])
